import numpy as np
import ml_dtypes


def mxq(x, axis, fmt="e4m3"):
    dtype, down = {"e4m3": (ml_dtypes.float8_e4m3fn, 7), "e5m2": (ml_dtypes.float8_e5m2, 14)}[fmt]
    v = np.moveaxis(np.asarray(x, np.float32).astype(ml_dtypes.bfloat16).astype(np.float64), axis, -1)
    blocks = v.reshape(v.shape[:-1] + (-1, 32))
    amax = np.abs(blocks).max(-1, keepdims=True)
    byte = np.maximum(np.where(amax > 0, np.frexp(amax)[1] - 1 + 127, 0) - down, 1)
    scale = np.exp2(byte - 127.0)
    codes = (blocks / scale).astype(np.float32).astype(dtype).astype(np.float64)
    return np.moveaxis((codes * scale).reshape(v.shape), -1, axis)


WIDE = False


def mx_kscale(k):
    if not WIDE:
        return np.ones(k)
    levels = np.array([10, -10, 5, -5, 0])
    if k % 512:
        return np.exp2(np.random.permutation(np.resize(levels, k // 32))).repeat(32)
    a = np.empty((k // 512, 16))
    for p in range(k // 512):
        a[p, :8] = np.random.permutation(np.resize(levels, 8))
        for g in range(8):
            far = levels[np.abs(levels - a[p, g]) >= 10]
            a[p, g + 8] = far[np.random.randint(len(far))]
    return np.exp2(a.ravel()).repeat(32)


def f64(x):
    return np.asarray(x).astype(np.float64)


def striped8(idx):
    return np.concatenate([v.reshape(-1, 16).T for v in idx]).astype(np.uint16)


def unstriped8(offs):
    return np.stack([offs[16 * g:16 * g + 16].T.reshape(-1) for g in range(8)]).astype(np.int64)


E2M1 = np.array([0.0, 0.5, 1.0, 1.5, 2.0, 3.0, 4.0, 6.0, -0.0, -0.5, -1.0, -1.5, -2.0, -3.0, -4.0, -6.0])


def pack_weight(w, fmt):
    k, n = w.shape
    w = f64(np.asarray(w, np.float32).astype(ml_dtypes.bfloat16)).reshape(k // 32, 32, n)
    amax = np.abs(w).max(1)
    if fmt == "e4m3":
        byte = np.frexp(amax)[1] - 1 + 127 - 7
    else:
        mant, ex = np.frexp(amax / 6.0)
        byte = np.where(mant > 0.5, ex, ex - 1) + 127
    byte = np.clip(np.where(amax > 0, byte, 1), 1, 254)
    scaled = (w * np.exp2(127.0 - byte)[:, None, :]).reshape(k, n).astype(np.float32)
    by_word = np.ascontiguousarray(scaled.reshape(k // 512, 128, 4, n).transpose(0, 1, 3, 2))
    if fmt == "e4m3":
        words = by_word.astype(ml_dtypes.float8_e4m3fn).view(np.uint8)
    else:
        c = by_word.astype(ml_dtypes.float4_e2m1fn).view(np.uint8) & 0xF
        words = (c[..., 0::2] | (c[..., 1::2] << 4)).reshape(k // 512, 128, 2 * n)
    return np.ascontiguousarray(words), np.ascontiguousarray(byte.astype(np.uint8).reshape(k // 512, 16, n))


def unpack_weight(words, scales, fmt):
    g, _, n = scales.shape
    words = np.ascontiguousarray(words).reshape(g, 128, n, -1)
    if fmt == "e4m3":
        vals = words.view(ml_dtypes.float8_e4m3fn).astype(np.float64)
    else:
        nib = np.empty((g, 128, n, 4), np.uint8)
        nib[..., 0::2] = words & 0xF
        nib[..., 1::2] = words >> 4
        vals = E2M1[nib]
    vals = vals * np.repeat(np.exp2(scales.astype(np.float64) - 127.0), 8, axis=1)[..., None]
    return vals.transpose(0, 1, 3, 2).reshape(g * 512, n)


def gelu(v):
    return 0.5 * v * (1.0 + np.tanh(np.sqrt(2.0 / np.pi) * (v + 0.044715 * v**3)))


K, M, T, S = 512, 1024, 1024, 512


def setup_inputs():
    n = np.random.standard_normal
    s = mx_kscale(K)[:, None]
    p_w = pack_weight(n((K, M)) / np.sqrt(K) / s, "e2m1")
    return {
        "xT": (n((K, T)) * s).astype(np.float32),
        "w_words": p_w[0],
        "w_scales": p_w[1],
        "wgt": np.repeat(np.random.uniform(0.5, 2.0, (8, S)), 16, axis=0).astype(np.float32),
        "b": (0.3 * n(1024)).astype(np.float32),
        "wgo": np.repeat(np.random.uniform(0.5, 2.0, (8, S)), 16, axis=0).astype(np.float32),
        "offs": striped8(np.stack([np.random.permutation(T)[:S] for _ in range(8)])),
        "offs2": striped8(np.stack([np.random.permutation(T)[:S] for _ in range(8)])),
    }


def reference(xT, w_words, w_scales, wgt, b, wgo, offs, offs2):
    idx = unstriped8(offs)
    group = np.arange(K) % 512 // 64
    xg = f64(wgt)[np.arange(K) // 4 % 128] * f64(xT)[np.arange(K)[:, None], idx[group]]
    xT_ = mxq(xg, 0, "e4m3")
    w_ = unpack_weight(w_words, w_scales, "e2m1")
    y = w_.T @ xT_
    place = unstriped8(offs2)[np.arange(M) % 128 // 16]
    out = np.zeros((M, T))
    out[np.arange(M)[:, None], place] = f64(wgo)[np.arange(M) % 128] * (gelu(y + f64(b)[:, None]))
    return out

@@ -1,0 +1,170 @@
+from contextlib import ExitStack
+
+import concourse.mybir as mybir
+from concourse.masks import make_identity
+
+K, M, T, S = 512, 1024, 1024, 512
+P = 128
+PACK = 4
+HALF = S // 2
+M_TILES = M // P
+FLOPS = 2 * K * M * S
+
+F32 = mybir.dt.float32
+BF16 = mybir.dt.bfloat16
+I32 = mybir.dt.int32
+U32 = mybir.dt.uint32
+U16 = mybir.dt.uint16
+U8 = mybir.dt.uint8
+FP8X4 = mybir.dt.float8_e4m3fn_x4
+FP4X4 = mybir.dt.float4_e2m1fn_x4
+MULT = mybir.AluOpType.mult
+GELU = mybir.ActivationFunctionType.Gelu_apprx_tanh
+
+
+def tile_list_hboth_gelu_kernel(tc, xT, w_words, w_scales, wgt, b, wgo, offs, offs2, out):
+    nc = tc.nc
+    with ExitStack() as ctx:
+        lists = ctx.enter_context(tc.tile_pool(name="lists", bufs=1))
+        keep = ctx.enter_context(tc.tile_pool(name="keep", bufs=1))
+        psum = ctx.enter_context(tc.psum_pool(name="psum", bufs=6))
+        turn = ctx.enter_context(tc.psum_pool(name="turn", bufs=1))
+
+        picks = lists.tile([P, S // 16], U16, name="picks")
+        places = lists.tile([P, S // 16], U16, name="places")
+        wgt_half = [keep.tile([P, HALF], F32, name=f"wgt{h}") for h in range(2)]
+        planes = [keep.tile([P, T], F32, name=f"plane{i}") for i in range(PACK)]
+        w_codes = keep.tile([P, 2 * M], U8, name="w_codes", align_bytes=64)
+        w_plane = keep.tile([P, M], U8, name="w_plane", align_bytes=64)
+        wgo_all = keep.tile([P, S], F32, name="wgo_all")
+        b_rows = keep.tile([P, P], F32, name="b_rows")
+        b_cols = keep.tile([P, M_TILES], F32, name="b_cols")
+        identity = keep.tile([P, P], F32, name="identity")
+        b_turned = turn.tile([P, P], F32, name="b_turned")
+        warm_in = keep.tile([P, 8], F32, name="warm_in")
+        warm_out = keep.tile([P, 8], F32, name="warm_out")
+        rows = [keep.tile([P, T], F32, name=f"rows{m}") for m in range(M_TILES)]
+
+        nc.vector.memset(b_rows[:], 0.0)
+        nc.scalar.dma_start(out=b_rows[0:M_TILES, :], in_=b.rearrange("(m p) -> m p", p=P))
+        nc.gpsimd.memset(w_plane[:].bitcast(I32), 0)
+        nc.vector.memset(warm_in[:], 0.0)
+        nc.scalar.activation(warm_out[:], warm_in[:], GELU)
+
+        x_planes = xT.rearrange("(p i) t -> p i t", i=PACK)
+        nc.sync.dma_start(picks[:], offs)
+        nc.sync.dma_start(out=wgt_half[0][:], in_=wgt[:, 0:HALF])
+        nc.sync.dma_start(out=planes[0][:], in_=x_planes[:, 0, :])
+        nc.sync.dma_start(out=wgt_half[1][:], in_=wgt[:, HALF:S])
+        for i in range(1, PACK):
+            nc.sync.dma_start(out=planes[i][:], in_=x_planes[:, i, :])
+        nc.sync.dma_start(out=w_codes[:].bitcast(I32), in_=w_words[0].bitcast(I32))
+        for q in range(4):
+            nc.sync.dma_start(
+                out=w_plane[32 * q : 32 * q + 4, :].bitcast(I32),
+                in_=w_scales[0, 4 * q : 4 * q + 4, :].bitcast(I32),
+            )
+        make_identity(nc, identity[:])
+        nc.tensor.transpose(b_turned[:], b_rows[:], identity[:])
+        nc.sync.dma_start(places[:], offs2)
+        nc.sync.dma_start(out=wgo_all[:], in_=wgo)
+
+        for m in range(M_TILES):
+            if m < 2:
+                nc.vector.memset(rows[m][:].bitcast(I32), 0)
+            else:
+                nc.gpsimd.memset(rows[m][:].bitcast(I32), 0)
+
+        codes = keep.tile([P, S], U32, name="codes", align_bytes=64)
+        scales = keep.tile([P, S], U8, name="scales", align_bytes=64)
+        grouped = [keep.tile([P, HALF, PACK], BF16, name=f"grouped{h}", align_bytes=64) for h in range(2)]
+        picked = {}
+        results = [keep.tile([P, S], F32, name=f"result{m}") for m in range(M_TILES)]
+
+        def half_list(tile, h):
+            return tile[:, h * HALF // 16 : (h + 1) * HALF // 16]
+
+        def gather(h, i):
+            if i % 2 == 0:
+                picked[h, i // 2] = keep.tile([P, 2, HALF], F32, name=f"picked{h}{i // 2}")
+            nc.vector.tensor_tensor(
+                picked[h, i // 2][:, i % 2, :],
+                planes[i][:].indirect(half_list(picks, h)),
+                wgt_half[h][:],
+                MULT,
+            )
+
+        def group(copy, h, pair):
+            copy(
+                out=grouped[h][:, :, 2 * pair : 2 * pair + 2],
+                in_=picked[h, pair][:].rearrange("p t c -> p c t"),
+            )
+
+        def quantize(h):
+            cols = slice(h * HALF, (h + 1) * HALF)
+            nc.vector.quantize_mx(
+                out=codes[:, cols].bitcast(FP8X4),
+                scales=scales[:, cols],
+                in_=grouped[h][:].rearrange("p c t -> p (c t)"),
+            )
+
+        def project(m, first, width):
+            cols = slice(first, first + width)
+            acc = psum.tile([P, width], F32, name="acc")
+            nc.tensor.matmul_mx(
+                out=acc[:],
+                lhsT=w_codes[:, 2 * P * m : 2 * P * (m + 1)].bitcast(FP4X4),
+                lhsT_scale=w_plane[:, P * m : P * (m + 1)],
+                rhs=codes[:, cols].bitcast(FP8X4),
+                rhs_scale=scales[:, cols],
+                start=True,
+                stop=True,
+            )
+            nc.scalar.activation(results[m][:, cols], acc[:], GELU, bias=b_cols[:, m : m + 1])
+
+        def place(m, h):
+            cols = slice(h * HALF, (h + 1) * HALF)
+            nc.vector.tensor_tensor(
+                rows[m][:].indirect(half_list(places, h)),
+                results[m][:, cols],
+                wgo_all[:, cols],
+                MULT,
+            )
+
+        def store(m):
+            nc.sync.dma_start(out=out[P * m : P * (m + 1), :], in_=rows[m][:])
+
+        vcopy, scopy = nc.vector.tensor_copy, nc.scalar.copy
+        gather(0, 0)
+        gather(1, 0)
+        gather(0, 1)
+        group(scopy, 0, 0)
+        gather(1, 1)
+        group(scopy, 1, 0)
+        nc.vector.tensor_copy(out=b_cols[:], in_=b_turned[:, 0:M_TILES])
+        gather(0, 2)
+        gather(1, 2)
+        gather(0, 3)
+        group(vcopy, 0, 1)
+        quantize(0)
+        project(0, 0, HALF)
+        gather(1, 3)
+        group(vcopy, 1, 1)
+        quantize(1)
+        project(1, 0, HALF)
+        place(0, 0)
+        place(1, 0)
+        project(0, HALF, HALF)
+        project(1, HALF, HALF)
+        place(0, 1)
+        store(0)
+        place(1, 1)
+        store(1)
+        for m in range(2, M_TILES, 2):
+            project(m, 0, S)
+            project(m + 1, 0, S)
+            for h in range(2):
+                place(m, h)
+                place(m + 1, h)
+            store(m)
+            store(m + 1)

@@ -7,6 +7,8 @@ K, M, T, S = 512, 1024, 1024, 512
 P = 128
 PACK = 4
 HALF = S // 2
+QUARTER = S // 4
+LATE_STEP = QUARTER + S
 M_TILES = M // P
 FLOPS = 2 * K * M * S
 
@@ -32,7 +34,8 @@ def tile_list_hboth_gelu_kernel(tc, xT, w_words, w_scales, wgt, b, wgo, offs, of
 
         picks = lists.tile([P, S // 16], U16, name="picks")
         places = lists.tile([P, S // 16], U16, name="places")
-        wgt_half = [keep.tile([P, HALF], F32, name=f"wgt{h}") for h in range(2)]
+        shared = keep.tile([P, 2 * LATE_STEP], F32, name="shared", align_bytes=64)
+        wgt_all = shared[:, QUARTER:LATE_STEP]
         planes = [keep.tile([P, T], F32, name=f"plane{i}") for i in range(PACK)]
         w_codes = keep.tile([P, 2 * M], U8, name="w_codes", align_bytes=64)
         w_plane = keep.tile([P, M], U8, name="w_plane", align_bytes=64)
@@ -53,17 +56,17 @@ def tile_list_hboth_gelu_kernel(tc, xT, w_words, w_scales, wgt, b, wgo, offs, of
 
         x_planes = xT.rearrange("(p i) t -> p i t", i=PACK)
         nc.sync.dma_start(picks[:], offs)
-        nc.sync.dma_start(out=wgt_half[0][:], in_=wgt[:, 0:HALF])
+        nc.sync.dma_start(out=wgt_all[:, 0:QUARTER], in_=wgt[:, 0:QUARTER])
         nc.sync.dma_start(out=planes[0][:], in_=x_planes[:, 0, :])
-        nc.sync.dma_start(out=wgt_half[1][:], in_=wgt[:, HALF:S])
+        nc.sync.dma_start(out=wgt_all[:, QUARTER:S], in_=wgt[:, QUARTER:S])
         for i in range(1, PACK):
             nc.sync.dma_start(out=planes[i][:], in_=x_planes[:, i, :])
-        nc.sync.dma_start(out=w_codes[:].bitcast(I32), in_=w_words[0].bitcast(I32))
         for q in range(4):
             nc.sync.dma_start(
                 out=w_plane[32 * q : 32 * q + 4, :].bitcast(I32),
                 in_=w_scales[0, 4 * q : 4 * q + 4, :].bitcast(I32),
             )
+        nc.sync.dma_start(out=w_codes[:].bitcast(I32), in_=w_words[0].bitcast(I32))
         make_identity(nc, identity[:])
         nc.tensor.transpose(b_turned[:], b_rows[:], identity[:])
         nc.sync.dma_start(places[:], offs2)
@@ -75,96 +78,93 @@ def tile_list_hboth_gelu_kernel(tc, xT, w_words, w_scales, wgt, b, wgo, offs, of
             else:
                 nc.gpsimd.memset(rows[m][:].bitcast(I32), 0)
 
+        first, second, third = slice(0, QUARTER), slice(QUARTER, HALF), slice(HALF, S)
+        front, rest, whole = slice(0, HALF), slice(QUARTER, S), slice(0, S)
         codes = keep.tile([P, S], U32, name="codes", align_bytes=64)
         scales = keep.tile([P, S], U8, name="scales", align_bytes=64)
-        grouped = [keep.tile([P, HALF, PACK], BF16, name=f"grouped{h}", align_bytes=64) for h in range(2)]
-        picked = {}
+        low = keep.tile([P, 2, S], F32, name="low")
+        high_front = keep.tile([P, 2, HALF], F32, name="high_front")
+        high_back = shared[:].rearrange("p (t c) -> p t c", t=2)[:, :, 0:HALF]
+        grouped_front = shared[:, LATE_STEP : LATE_STEP + 2 * HALF].bitcast(BF16)
+        grouped_third = keep.tile([P, HALF * PACK], BF16, name="grouped_third", align_bytes=64)
+        grouped = {
+            (first.start, first.stop): grouped_front[:, 0 : QUARTER * PACK],
+            (second.start, second.stop): grouped_front[:, QUARTER * PACK : HALF * PACK],
+            (front.start, front.stop): grouped_front,
+            (third.start, third.stop): grouped_third[:],
+        }
         results = [keep.tile([P, S], F32, name=f"result{m}") for m in range(M_TILES)]
 
-        def half_list(tile, h):
-            return tile[:, h * HALF // 16 : (h + 1) * HALF // 16]
+        def entries(tile, cols):
+            return tile[:, cols.start // 16 : cols.stop // 16]
 
-        def gather(h, i):
-            if i % 2 == 0:
-                picked[h, i // 2] = keep.tile([P, 2, HALF], F32, name=f"picked{h}{i // 2}")
-            nc.vector.tensor_tensor(
-                picked[h, i // 2][:, i % 2, :],
-                planes[i][:].indirect(half_list(picks, h)),
-                wgt_half[h][:],
-                MULT,
+        def gather(i, cols, dst):
+            nc.vector.tensor_tensor(dst, planes[i][:].indirect(entries(picks, cols)), wgt_all[:, cols], MULT)
+
+        def group(cols, pair, src):
+            nc.scalar.copy(
+                out=grouped[cols.start, cols.stop].rearrange("p (c t) -> p c t", t=PACK)[:, :, 2 * pair : 2 * pair + 2],
+                in_=src.rearrange("p t c -> p c t"),
             )
 
-        def group(copy, h, pair):
-            copy(
-                out=grouped[h][:, :, 2 * pair : 2 * pair + 2],
-                in_=picked[h, pair][:].rearrange("p t c -> p c t"),
-            )
+        def quantize(cols):
+            nc.vector.quantize_mx(out=codes[:, cols].bitcast(FP8X4), scales=scales[:, cols], in_=grouped[cols.start, cols.stop])
 
-        def quantize(h):
-            cols = slice(h * HALF, (h + 1) * HALF)
-            nc.vector.quantize_mx(
-                out=codes[:, cols].bitcast(FP8X4),
-                scales=scales[:, cols],
-                in_=grouped[h][:].rearrange("p c t -> p (c t)"),
-            )
+        def project(m, parts, result, bias=None):
+            start, stop = parts[0].start, parts[-1].stop
+            acc = psum.tile([P, stop - start], F32, name="acc")
+            for cols in parts:
+                nc.tensor.matmul_mx(
+                    out=acc[:, cols.start - start : cols.stop - start],
+                    lhsT=w_codes[:, 2 * P * m : 2 * P * (m + 1)].bitcast(FP4X4),
+                    lhsT_scale=w_plane[:, P * m : P * (m + 1)],
+                    rhs=codes[:, cols].bitcast(FP8X4),
+                    rhs_scale=scales[:, cols],
+                    start=True,
+                    stop=True,
+                )
+            nc.scalar.activation(result, acc[:], GELU, bias=b_cols[:, m : m + 1] if bias is None else bias)
 
-        def project(m, first, width):
-            cols = slice(first, first + width)
-            acc = psum.tile([P, width], F32, name="acc")
-            nc.tensor.matmul_mx(
-                out=acc[:],
-                lhsT=w_codes[:, 2 * P * m : 2 * P * (m + 1)].bitcast(FP4X4),
-                lhsT_scale=w_plane[:, P * m : P * (m + 1)],
-                rhs=codes[:, cols].bitcast(FP8X4),
-                rhs_scale=scales[:, cols],
-                start=True,
-                stop=True,
-            )
-            nc.scalar.activation(results[m][:, cols], acc[:], GELU, bias=b_cols[:, m : m + 1])
-
-        def place(m, h):
-            cols = slice(h * HALF, (h + 1) * HALF)
-            nc.vector.tensor_tensor(
-                rows[m][:].indirect(half_list(places, h)),
-                results[m][:, cols],
-                wgo_all[:, cols],
-                MULT,
-            )
+        def place(m, cols, result):
+            nc.vector.tensor_tensor(rows[m][:].indirect(entries(places, cols)), result, wgo_all[:, cols], MULT)
 
         def store(m):
             nc.sync.dma_start(out=out[P * m : P * (m + 1), :], in_=rows[m][:])
 
-        vcopy, scopy = nc.vector.tensor_copy, nc.scalar.copy
-        gather(0, 0)
-        gather(1, 0)
-        gather(0, 1)
-        group(scopy, 0, 0)
-        gather(1, 1)
-        group(scopy, 1, 0)
-        nc.vector.tensor_copy(out=b_cols[:], in_=b_turned[:, 0:M_TILES])
-        gather(0, 2)
-        gather(1, 2)
-        gather(0, 3)
-        group(vcopy, 0, 1)
-        quantize(0)
-        project(0, 0, HALF)
-        gather(1, 3)
-        group(vcopy, 1, 1)
-        quantize(1)
-        project(1, 0, HALF)
-        place(0, 0)
-        place(1, 0)
-        project(0, HALF, HALF)
-        project(1, HALF, HALF)
-        place(0, 1)
-        store(0)
-        place(1, 1)
-        store(1)
-        for m in range(2, M_TILES, 2):
-            project(m, 0, S)
-            project(m + 1, 0, S)
-            for h in range(2):
-                place(m, h)
-                place(m + 1, h)
+        gather(0, first, low[:, 0, first])
+        gather(0, rest, low[:, 0, rest])
+        gather(1, whole, low[:, 1, :])
+        group(front, 0, low[:, :, front])
+        group(third, 0, low[:, :, third])
+        nc.scalar.copy(out=b_cols[:], in_=b_turned[:, 0:M_TILES])
+        first_bias = grouped_third[:].bitcast(F32)[:, 1:2]
+        nc.scalar.copy(out=first_bias, in_=b_turned[:, 0:1])
+        gather(2, front, high_front[:, 0, :])
+        gather(3, first, high_front[:, 1, first])
+        group(first, 1, high_front[:, :, first])
+        gather(3, second, high_front[:, 1, second])
+        group(second, 1, high_front[:, :, second])
+        gather(2, third, shared[:, 0:HALF])
+        quantize(first)
+        project(0, [first], results[0][:, first], first_bias)
+        project(1, [first], results[1][:, first])
+        quantize(second)
+        gather(3, third, shared[:, LATE_STEP : LATE_STEP + HALF])
+        place(0, first, results[0][:, first])
+        place(1, first, results[1][:, first])
+        group(third, 1, high_back)
+        quantize(third)
+        late_result = shared[:, LATE_STEP : LATE_STEP + HALF]
+        project(2, [front], late_result)
+        place(2, front, late_result)
+        for m in range(2):
+            project(m, [second, third], results[m][:, rest])
+            place(m, rest, results[m][:, rest])
             store(m)
-            store(m + 1)
+        project(2, [third], results[2][:, third])
+        place(2, third, results[2][:, third])
+        store(2)
+        for m in range(3, M_TILES):
+            project(m, [whole], results[m][:])
+            place(m, whole, results[m][:])
+            store(m)

@@ -8,8 +8,9 @@ P = 128
 PACK = 4
 HALF = S // 2
 QUARTER = S // 4
-LATE_STEP = QUARTER + S
+LATE_STEP = QUARTER + S + HALF
 M_TILES = M // P
+PAGES = 4
 FLOPS = 2 * K * M * S
 
 F32 = mybir.dt.float32
@@ -29,13 +30,14 @@ def tile_list_hboth_gelu_kernel(tc, xT, w_words, w_scales, wgt, b, wgo, offs, of
     with ExitStack() as ctx:
         lists = ctx.enter_context(tc.tile_pool(name="lists", bufs=1))
         keep = ctx.enter_context(tc.tile_pool(name="keep", bufs=1))
+        pages = ctx.enter_context(tc.tile_pool(name="pages", bufs=PAGES))
         psum = ctx.enter_context(tc.psum_pool(name="psum", bufs=6))
         turn = ctx.enter_context(tc.psum_pool(name="turn", bufs=1))
 
         picks = lists.tile([P, S // 16], U16, name="picks")
         places = lists.tile([P, S // 16], U16, name="places")
         shared = keep.tile([P, 2 * LATE_STEP], F32, name="shared", align_bytes=64)
-        wgt_all = shared[:, QUARTER:LATE_STEP]
+        wgt_all = shared[:, QUARTER : QUARTER + S]
         planes = [keep.tile([P, T], F32, name=f"plane{i}") for i in range(PACK)]
         w_codes = keep.tile([P, 2 * M], U8, name="w_codes", align_bytes=64)
         w_plane = keep.tile([P, M], U8, name="w_plane", align_bytes=64)
@@ -46,7 +48,7 @@ def tile_list_hboth_gelu_kernel(tc, xT, w_words, w_scales, wgt, b, wgo, offs, of
         b_turned = turn.tile([P, P], F32, name="b_turned")
         warm_in = keep.tile([P, 8], F32, name="warm_in")
         warm_out = keep.tile([P, 8], F32, name="warm_out")
-        rows = [keep.tile([P, T], F32, name=f"rows{m}") for m in range(M_TILES)]
+        rows = {}
 
         nc.vector.memset(b_rows[:], 0.0)
         nc.scalar.dma_start(out=b_rows[0:M_TILES, :], in_=b.rearrange("(m p) -> m p", p=P))
@@ -72,25 +74,26 @@ def tile_list_hboth_gelu_kernel(tc, xT, w_words, w_scales, wgt, b, wgo, offs, of
         nc.sync.dma_start(places[:], offs2)
         nc.sync.dma_start(out=wgo_all[:], in_=wgo)
 
-        for m in range(M_TILES):
-            if m < 2:
-                nc.vector.memset(rows[m][:].bitcast(I32), 0)
-            else:
-                nc.gpsimd.memset(rows[m][:].bitcast(I32), 0)
+        def clear(m, engine):
+            rows[m] = pages.tile([P, T], F32, name="rows")
+            engine.memset(rows[m][:].bitcast(I32), 0)
+
+        for m in range(PAGES):
+            clear(m, nc.vector if m < 2 else nc.gpsimd)
 
         first, second, third = slice(0, QUARTER), slice(QUARTER, HALF), slice(HALF, S)
         front, rest, whole = slice(0, HALF), slice(QUARTER, S), slice(0, S)
         codes = keep.tile([P, S], U32, name="codes", align_bytes=64)
         scales = keep.tile([P, S], U8, name="scales", align_bytes=64)
         low = keep.tile([P, 2, S], F32, name="low")
-        high_front = keep.tile([P, 2, HALF], F32, name="high_front")
+        high_front = shared[:, LATE_STEP - HALF : LATE_STEP + HALF].rearrange("p (t c) -> p t c", t=2)
         high_back = shared[:].rearrange("p (t c) -> p t c", t=2)[:, :, 0:HALF]
-        grouped_front = shared[:, LATE_STEP : LATE_STEP + 2 * HALF].bitcast(BF16)
+        grouped_front = keep.tile([P, HALF * PACK], BF16, name="grouped_front", align_bytes=64)
         grouped_third = keep.tile([P, HALF * PACK], BF16, name="grouped_third", align_bytes=64)
         grouped = {
             (first.start, first.stop): grouped_front[:, 0 : QUARTER * PACK],
             (second.start, second.stop): grouped_front[:, QUARTER * PACK : HALF * PACK],
-            (front.start, front.stop): grouped_front,
+            (front.start, front.stop): grouped_front[:],
             (third.start, third.stop): grouped_third[:],
         }
         results = [keep.tile([P, S], F32, name=f"result{m}") for m in range(M_TILES)]
@@ -130,6 +133,8 @@ def tile_list_hboth_gelu_kernel(tc, xT, w_words, w_scales, wgt, b, wgo, offs, of
 
         def store(m):
             nc.sync.dma_start(out=out[P * m : P * (m + 1), :], in_=rows[m][:])
+            if m + PAGES < M_TILES:
+                clear(m + PAGES, nc.gpsimd)
 
         gather(0, first, low[:, 0, first])
         gather(0, rest, low[:, 0, rest])

@@ -10,7 +10,6 @@ HALF = S // 2
 QUARTER = S // 4
 LATE_STEP = QUARTER + S + HALF
 M_TILES = M // P
-PAGES = 4
 FLOPS = 2 * K * M * S
 
 F32 = mybir.dt.float32
@@ -30,7 +29,6 @@ def tile_list_hboth_gelu_kernel(tc, xT, w_words, w_scales, wgt, b, wgo, offs, of
     with ExitStack() as ctx:
         lists = ctx.enter_context(tc.tile_pool(name="lists", bufs=1))
         keep = ctx.enter_context(tc.tile_pool(name="keep", bufs=1))
-        pages = ctx.enter_context(tc.tile_pool(name="pages", bufs=PAGES))
         psum = ctx.enter_context(tc.psum_pool(name="psum", bufs=6))
         turn = ctx.enter_context(tc.psum_pool(name="turn", bufs=1))
 
@@ -48,7 +46,7 @@ def tile_list_hboth_gelu_kernel(tc, xT, w_words, w_scales, wgt, b, wgo, offs, of
         b_turned = turn.tile([P, P], F32, name="b_turned")
         warm_in = keep.tile([P, 8], F32, name="warm_in")
         warm_out = keep.tile([P, 8], F32, name="warm_out")
-        rows = {}
+        rows = [keep.tile([P, T], F32, name=f"rows{m}") for m in range(M_TILES)]
 
         nc.vector.memset(b_rows[:], 0.0)
         nc.scalar.dma_start(out=b_rows[0:M_TILES, :], in_=b.rearrange("(m p) -> m p", p=P))
@@ -57,9 +55,9 @@ def tile_list_hboth_gelu_kernel(tc, xT, w_words, w_scales, wgt, b, wgo, offs, of
         nc.scalar.activation(warm_out[:], warm_in[:], GELU)
 
         x_planes = xT.rearrange("(p i) t -> p i t", i=PACK)
+        nc.sync.dma_start(out=planes[0][:], in_=x_planes[:, 0, :])
         nc.sync.dma_start(picks[:], offs)
         nc.sync.dma_start(out=wgt_all[:, 0:QUARTER], in_=wgt[:, 0:QUARTER])
-        nc.sync.dma_start(out=planes[0][:], in_=x_planes[:, 0, :])
         nc.sync.dma_start(out=wgt_all[:, QUARTER:S], in_=wgt[:, QUARTER:S])
         for i in range(1, PACK):
             nc.sync.dma_start(out=planes[i][:], in_=x_planes[:, i, :])
@@ -74,12 +72,11 @@ def tile_list_hboth_gelu_kernel(tc, xT, w_words, w_scales, wgt, b, wgo, offs, of
         nc.sync.dma_start(places[:], offs2)
         nc.sync.dma_start(out=wgo_all[:], in_=wgo)
 
-        def clear(m, engine):
-            rows[m] = pages.tile([P, T], F32, name="rows")
-            engine.memset(rows[m][:].bitcast(I32), 0)
-
-        for m in range(PAGES):
-            clear(m, nc.vector if m < 2 else nc.gpsimd)
+        for m in range(M_TILES):
+            if m < 2:
+                nc.vector.memset(rows[m][:].bitcast(I32), 0)
+            else:
+                nc.gpsimd.memset(rows[m][:].bitcast(I32), 0)
 
         first, second, third = slice(0, QUARTER), slice(QUARTER, HALF), slice(HALF, S)
         front, rest, whole = slice(0, HALF), slice(QUARTER, S), slice(0, S)
@@ -133,13 +130,12 @@ def tile_list_hboth_gelu_kernel(tc, xT, w_words, w_scales, wgt, b, wgo, offs, of
 
         def store(m):
             nc.sync.dma_start(out=out[P * m : P * (m + 1), :], in_=rows[m][:])
-            if m + PAGES < M_TILES:
-                clear(m + PAGES, nc.gpsimd)
 
         gather(0, first, low[:, 0, first])
         gather(0, rest, low[:, 0, rest])
-        gather(1, whole, low[:, 1, :])
+        gather(1, front, low[:, 1, front])
         group(front, 0, low[:, :, front])
+        gather(1, third, low[:, 1, third])
         group(third, 0, low[:, :, third])
         nc.scalar.copy(out=b_cols[:], in_=b_turned[:, 0:M_TILES])
         first_bias = grouped_third[:].bitcast(F32)[:, 1:2]

@@ -44,15 +44,13 @@ def tile_list_hboth_gelu_kernel(tc, xT, w_words, w_scales, wgt, b, wgo, offs, of
         b_cols = keep.tile([P, M_TILES], F32, name="b_cols")
         identity = keep.tile([P, P], F32, name="identity")
         b_turned = turn.tile([P, P], F32, name="b_turned")
-        warm_in = keep.tile([P, 8], F32, name="warm_in")
         warm_out = keep.tile([P, 8], F32, name="warm_out")
         rows = [keep.tile([P, T], F32, name=f"rows{m}") for m in range(M_TILES)]
 
         nc.vector.memset(b_rows[:], 0.0)
         nc.scalar.dma_start(out=b_rows[0:M_TILES, :], in_=b.rearrange("(m p) -> m p", p=P))
+        nc.scalar.activation(warm_out[64:P, :], b_rows[64:P, 0:8], GELU)
         nc.gpsimd.memset(w_plane[:].bitcast(I32), 0)
-        nc.vector.memset(warm_in[:], 0.0)
-        nc.scalar.activation(warm_out[:], warm_in[:], GELU)
 
         x_planes = xT.rearrange("(p i) t -> p i t", i=PACK)
         nc.sync.dma_start(out=planes[0][:], in_=x_planes[:, 0, :])
@@ -83,7 +81,9 @@ def tile_list_hboth_gelu_kernel(tc, xT, w_words, w_scales, wgt, b, wgo, offs, of
         codes = keep.tile([P, S], U32, name="codes", align_bytes=64)
         scales = keep.tile([P, S], U8, name="scales", align_bytes=64)
         low = keep.tile([P, 2, S], F32, name="low")
-        high_front = shared[:, LATE_STEP - HALF : LATE_STEP + HALF].rearrange("p (t c) -> p t c", t=2)
+        mid = LATE_STEP - HALF
+        high_first = shared[:, mid : mid + 2 * HALF].rearrange("p (t c) -> p t c", t=2)[:, :, 0:QUARTER]
+        high_second = shared[:, mid + QUARTER : mid + QUARTER + 6 * QUARTER].rearrange("p (t c) -> p t c", t=2)[:, :, 0:QUARTER]
         high_back = shared[:].rearrange("p (t c) -> p t c", t=2)[:, :, 0:HALF]
         grouped_front = keep.tile([P, HALF * PACK], BF16, name="grouped_front", align_bytes=64)
         grouped_third = keep.tile([P, HALF * PACK], BF16, name="grouped_third", align_bytes=64)
@@ -140,17 +140,18 @@ def tile_list_hboth_gelu_kernel(tc, xT, w_words, w_scales, wgt, b, wgo, offs, of
         nc.scalar.copy(out=b_cols[:], in_=b_turned[:, 0:M_TILES])
         first_bias = grouped_third[:].bitcast(F32)[:, 1:2]
         nc.scalar.copy(out=first_bias, in_=b_turned[:, 0:1])
-        gather(2, front, high_front[:, 0, :])
-        gather(3, first, high_front[:, 1, first])
-        group(first, 1, high_front[:, :, first])
-        gather(3, second, high_front[:, 1, second])
-        group(second, 1, high_front[:, :, second])
-        gather(2, third, shared[:, 0:HALF])
+        gather(2, front, shared[:, mid:LATE_STEP])
+        gather(2, slice(HALF, HALF + QUARTER), shared[:, 0:QUARTER])
+        gather(3, first, high_first[:, 1, :])
+        group(first, 1, high_first)
+        gather(3, second, high_second[:, 1, :])
+        group(second, 1, high_second)
+        gather(2, slice(HALF + QUARTER, S), shared[:, QUARTER:HALF])
         quantize(first)
         project(0, [first], results[0][:, first], first_bias)
+        gather(3, third, shared[:, LATE_STEP : LATE_STEP + HALF])
         project(1, [first], results[1][:, first])
         quantize(second)
-        gather(3, third, shared[:, LATE_STEP : LATE_STEP + HALF])
         place(0, first, results[0][:, first])
         place(1, first, results[1][:, first])
         group(third, 1, high_back)

@@ -8,7 +8,7 @@ P = 128
 PACK = 4
 HALF = S // 2
 QUARTER = S // 4
-LATE_STEP = QUARTER + S + HALF
+OVERHANG = 8
 M_TILES = M // P
 FLOPS = 2 * K * M * S
 
@@ -34,8 +34,7 @@ def tile_list_hboth_gelu_kernel(tc, xT, w_words, w_scales, wgt, b, wgo, offs, of
 
         picks = lists.tile([P, S // 16], U16, name="picks")
         places = lists.tile([P, S // 16], U16, name="places")
-        shared = keep.tile([P, 2 * LATE_STEP], F32, name="shared", align_bytes=64)
-        wgt_all = shared[:, QUARTER : QUARTER + S]
+        wgt_all = keep.tile([P, S], F32, name="wgt_all")
         planes = [keep.tile([P, T], F32, name=f"plane{i}") for i in range(PACK)]
         w_codes = keep.tile([P, 2 * M], U8, name="w_codes", align_bytes=64)
         w_plane = keep.tile([P, M], U8, name="w_plane", align_bytes=64)
@@ -47,18 +46,21 @@ def tile_list_hboth_gelu_kernel(tc, xT, w_words, w_scales, wgt, b, wgo, offs, of
         warm_out = keep.tile([P, 8], F32, name="warm_out")
         rows = [keep.tile([P, T], F32, name=f"rows{m}") for m in range(M_TILES)]
 
-        nc.vector.memset(b_rows[:], 0.0)
+        nc.gpsimd.memset(b_rows[:], 0.0)
         nc.scalar.dma_start(out=b_rows[0:M_TILES, :], in_=b.rearrange("(m p) -> m p", p=P))
         nc.scalar.activation(warm_out[64:P, :], b_rows[64:P, 0:8], GELU)
         nc.gpsimd.memset(w_plane[:].bitcast(I32), 0)
 
+        first, middle, last = slice(0, QUARTER), slice(QUARTER, S - QUARTER), slice(S - QUARTER, S)
+        early, rest, whole = slice(0, S - QUARTER), slice(QUARTER, S), slice(0, S)
+
         x_planes = xT.rearrange("(p i) t -> p i t", i=PACK)
         nc.sync.dma_start(out=planes[0][:], in_=x_planes[:, 0, :])
         nc.sync.dma_start(picks[:], offs)
-        nc.sync.dma_start(out=wgt_all[:, 0:QUARTER], in_=wgt[:, 0:QUARTER])
-        nc.sync.dma_start(out=wgt_all[:, QUARTER:S], in_=wgt[:, QUARTER:S])
+        nc.sync.dma_start(out=wgt_all[:, early], in_=wgt[:, early])
         for i in range(1, PACK):
             nc.sync.dma_start(out=planes[i][:], in_=x_planes[:, i, :])
+        nc.sync.dma_start(out=wgt_all[:, last], in_=wgt[:, last])
         for q in range(4):
             nc.sync.dma_start(
                 out=w_plane[32 * q : 32 * q + 4, :].bitcast(I32),
@@ -67,8 +69,8 @@ def tile_list_hboth_gelu_kernel(tc, xT, w_words, w_scales, wgt, b, wgo, offs, of
         nc.sync.dma_start(out=w_codes[:].bitcast(I32), in_=w_words[0].bitcast(I32))
         make_identity(nc, identity[:])
         nc.tensor.transpose(b_turned[:], b_rows[:], identity[:])
-        nc.sync.dma_start(places[:], offs2)
         nc.sync.dma_start(out=wgo_all[:], in_=wgo)
+        nc.sync.dma_start(places[:], offs2)
 
         for m in range(M_TILES):
             if m < 2:
@@ -76,24 +78,21 @@ def tile_list_hboth_gelu_kernel(tc, xT, w_words, w_scales, wgt, b, wgo, offs, of
             else:
                 nc.gpsimd.memset(rows[m][:].bitcast(I32), 0)
 
-        first, second, third = slice(0, QUARTER), slice(QUARTER, HALF), slice(HALF, S)
-        front, rest, whole = slice(0, HALF), slice(QUARTER, S), slice(0, S)
         codes = keep.tile([P, S], U32, name="codes", align_bytes=64)
         scales = keep.tile([P, S], U8, name="scales", align_bytes=64)
-        low = keep.tile([P, 2, S], F32, name="low")
-        mid = LATE_STEP - HALF
-        high_first = shared[:, mid : mid + 2 * HALF].rearrange("p (t c) -> p t c", t=2)[:, :, 0:QUARTER]
-        high_second = shared[:, mid + QUARTER : mid + QUARTER + 6 * QUARTER].rearrange("p (t c) -> p t c", t=2)[:, :, 0:QUARTER]
-        high_back = shared[:].rearrange("p (t c) -> p t c", t=2)[:, :, 0:HALF]
-        grouped_front = keep.tile([P, HALF * PACK], BF16, name="grouped_front", align_bytes=64)
-        grouped_third = keep.tile([P, HALF * PACK], BF16, name="grouped_third", align_bytes=64)
-        grouped = {
-            (first.start, first.stop): grouped_front[:, 0 : QUARTER * PACK],
-            (second.start, second.stop): grouped_front[:, QUARTER * PACK : HALF * PACK],
-            (front.start, front.stop): grouped_front[:],
-            (third.start, third.stop): grouped_third[:],
-        }
+        low = keep.tile([P, 2, S - QUARTER], F32, name="low")
+        high_middle = keep.tile([P, 2, HALF], F32, name="high_middle")
+        reused = keep.tile([P, S], F32, name="reused")
+        high_first = reused[:, 0 : 2 * (QUARTER + OVERHANG)].rearrange("p (t c) -> p t c", t=2)[:, :, 0:QUARTER]
+        picked_last = reused[:].rearrange("p (t c) -> p t c", t=PACK)
+        grouped_early = keep.tile([P, (S - QUARTER) * PACK], BF16, name="grouped_early", align_bytes=64)
+        grouped_last = keep.tile([P, QUARTER * PACK], BF16, name="grouped_last", align_bytes=64)
         results = [keep.tile([P, S], F32, name=f"result{m}") for m in range(M_TILES)]
+
+        def grouped(cols):
+            if cols == last:
+                return grouped_last[:]
+            return grouped_early[:, cols.start * PACK : cols.stop * PACK]
 
         def entries(tile, cols):
             return tile[:, cols.start // 16 : cols.stop // 16]
@@ -101,16 +100,16 @@ def tile_list_hboth_gelu_kernel(tc, xT, w_words, w_scales, wgt, b, wgo, offs, of
         def gather(i, cols, dst):
             nc.vector.tensor_tensor(dst, planes[i][:].indirect(entries(picks, cols)), wgt_all[:, cols], MULT)
 
-        def group(cols, pair, src):
+        def group(cols, which, src):
             nc.scalar.copy(
-                out=grouped[cols.start, cols.stop].rearrange("p (c t) -> p c t", t=PACK)[:, :, 2 * pair : 2 * pair + 2],
+                out=grouped(cols).rearrange("p (c t) -> p c t", t=PACK)[:, :, which],
                 in_=src.rearrange("p t c -> p c t"),
             )
 
         def quantize(cols):
-            nc.vector.quantize_mx(out=codes[:, cols].bitcast(FP8X4), scales=scales[:, cols], in_=grouped[cols.start, cols.stop])
+            nc.vector.quantize_mx(out=codes[:, cols].bitcast(FP8X4), scales=scales[:, cols], in_=grouped(cols))
 
-        def project(m, parts, result, bias=None):
+        def project(m, parts, result, bias):
             start, stop = parts[0].start, parts[-1].stop
             acc = psum.tile([P, stop - start], F32, name="acc")
             for cols in parts:
@@ -123,7 +122,7 @@ def tile_list_hboth_gelu_kernel(tc, xT, w_words, w_scales, wgt, b, wgo, offs, of
                     start=True,
                     stop=True,
                 )
-            nc.scalar.activation(result, acc[:], GELU, bias=b_cols[:, m : m + 1] if bias is None else bias)
+            nc.scalar.activation(result, acc[:], GELU, bias=bias)
 
         def place(m, cols, result):
             nc.vector.tensor_tensor(rows[m][:].indirect(entries(places, cols)), result, wgo_all[:, cols], MULT)
@@ -131,42 +130,40 @@ def tile_list_hboth_gelu_kernel(tc, xT, w_words, w_scales, wgt, b, wgo, offs, of
         def store(m):
             nc.sync.dma_start(out=out[P * m : P * (m + 1), :], in_=rows[m][:])
 
-        gather(0, first, low[:, 0, first])
-        gather(0, rest, low[:, 0, rest])
-        gather(1, front, low[:, 1, front])
-        group(front, 0, low[:, :, front])
-        gather(1, third, low[:, 1, third])
-        group(third, 0, low[:, :, third])
+        low_pair, high_pair, all_four = slice(0, 2), slice(2, PACK), slice(0, PACK)
         nc.scalar.copy(out=b_cols[:], in_=b_turned[:, 0:M_TILES])
-        first_bias = grouped_third[:].bitcast(F32)[:, 1:2]
-        nc.scalar.copy(out=first_bias, in_=b_turned[:, 0:1])
-        gather(2, front, shared[:, mid:LATE_STEP])
-        gather(2, slice(HALF, HALF + QUARTER), shared[:, 0:QUARTER])
+        first_bias = grouped_last[:].bitcast(F32)[:, 0:2]
+        nc.scalar.copy(out=first_bias, in_=b_turned[:, 0:2])
+        gather(0, early, low[:, 0, :])
+        gather(1, early, low[:, 1, :])
+        group(early, low_pair, low[:])
+        gather(2, first, high_first[:, 0, :])
+        gather(2, middle, high_middle[:, 0, :])
         gather(3, first, high_first[:, 1, :])
-        group(first, 1, high_first)
-        gather(3, second, high_second[:, 1, :])
-        group(second, 1, high_second)
-        gather(2, slice(HALF + QUARTER, S), shared[:, QUARTER:HALF])
+        group(first, high_pair, high_first)
+        gather(3, middle, high_middle[:, 1, :])
+        group(middle, high_pair, high_middle[:])
+        gather(3, last, picked_last[:, 3, :])
         quantize(first)
-        project(0, [first], results[0][:, first], first_bias)
-        gather(3, third, shared[:, LATE_STEP : LATE_STEP + HALF])
-        project(1, [first], results[1][:, first])
-        quantize(second)
-        place(0, first, results[0][:, first])
-        place(1, first, results[1][:, first])
-        group(third, 1, high_back)
-        quantize(third)
-        late_result = shared[:, LATE_STEP : LATE_STEP + HALF]
-        project(2, [front], late_result)
-        place(2, front, late_result)
         for m in range(2):
-            project(m, [second, third], results[m][:, rest])
+            project(m, [first], results[m][:, first], first_bias[:, m : m + 1])
+        for i in range(3):
+            gather(i, last, picked_last[:, i, :])
+        quantize(middle)
+        for m in range(2):
+            place(m, first, results[m][:, first])
+        group(last, all_four, picked_last)
+        quantize(last)
+        project(2, [first, middle], reused[:, early], b_cols[:, 2:3])
+        place(2, early, reused[:, early])
+        for m in range(2):
+            project(m, [middle, last], results[m][:, rest], b_cols[:, m : m + 1])
             place(m, rest, results[m][:, rest])
             store(m)
-        project(2, [third], results[2][:, third])
-        place(2, third, results[2][:, third])
+        project(2, [last], results[2][:, last], b_cols[:, 2:3])
+        place(2, last, results[2][:, last])
         store(2)
         for m in range(3, M_TILES):
-            project(m, [whole], results[m][:])
+            project(m, [whole], results[m][:], b_cols[:, m : m + 1])
             place(m, whole, results[m][:])
             store(m)

@@ -53,6 +53,7 @@ def tile_list_hboth_gelu_kernel(tc, xT, w_words, w_scales, wgt, b, wgo, offs, of
 
         first, middle, last = slice(0, QUARTER), slice(QUARTER, S - QUARTER), slice(S - QUARTER, S)
         early, rest, whole = slice(0, S - QUARTER), slice(QUARTER, S), slice(0, S)
+        front, back, third = slice(0, HALF), slice(HALF, S), slice(HALF, S - QUARTER)
 
         x_planes = xT.rearrange("(p i) t -> p i t", i=PACK)
         nc.sync.dma_start(out=planes[0][:], in_=x_planes[:, 0, :])
@@ -82,6 +83,7 @@ def tile_list_hboth_gelu_kernel(tc, xT, w_words, w_scales, wgt, b, wgo, offs, of
         scales = keep.tile([P, S], U8, name="scales", align_bytes=64)
         low = keep.tile([P, 2, S - QUARTER], F32, name="low")
         high_middle = keep.tile([P, 2, HALF], F32, name="high_middle")
+        unweighted = keep.tile([P, HALF], F32, name="unweighted")
         reused = keep.tile([P, S], F32, name="reused")
         high_first = reused[:, 0 : 2 * (QUARTER + OVERHANG)].rearrange("p (t c) -> p t c", t=2)[:, :, 0:QUARTER]
         picked_last = reused[:].rearrange("p (t c) -> p t c", t=PACK)
@@ -99,6 +101,9 @@ def tile_list_hboth_gelu_kernel(tc, xT, w_words, w_scales, wgt, b, wgo, offs, of
 
         def gather(i, cols, dst):
             nc.vector.tensor_tensor(dst, planes[i][:].indirect(entries(picks, cols)), wgt_all[:, cols], MULT)
+
+        def weigh(cols, dst):
+            nc.vector.tensor_tensor(dst, unweighted[:, cols.start - HALF : cols.stop - HALF], wgt_all[:, cols], MULT)
 
         def group(cols, which, src):
             nc.scalar.copy(
@@ -134,7 +139,9 @@ def tile_list_hboth_gelu_kernel(tc, xT, w_words, w_scales, wgt, b, wgo, offs, of
         nc.scalar.copy(out=b_cols[:], in_=b_turned[:, 0:M_TILES])
         first_bias = grouped_last[:].bitcast(F32)[:, 0:2]
         nc.scalar.copy(out=first_bias, in_=b_turned[:, 0:2])
-        gather(0, early, low[:, 0, :])
+        nc.vector.tensor_copy(unweighted[:], planes[0][:].indirect(entries(picks, back)))
+        gather(0, front, low[:, 0, front])
+        weigh(third, low[:, 0, third])
         gather(1, early, low[:, 1, :])
         group(early, low_pair, low[:])
         gather(2, first, high_first[:, 0, :])
@@ -147,8 +154,9 @@ def tile_list_hboth_gelu_kernel(tc, xT, w_words, w_scales, wgt, b, wgo, offs, of
         quantize(first)
         for m in range(2):
             project(m, [first], results[m][:, first], first_bias[:, m : m + 1])
-        for i in range(3):
+        for i in range(1, 3):
             gather(i, last, picked_last[:, i, :])
+        weigh(last, picked_last[:, 0, :])
         quantize(middle)
         for m in range(2):
             place(m, first, results[m][:, first])

@@ -9,6 +9,8 @@ PACK = 4
 HALF = S // 2
 QUARTER = S // 4
 OVERHANG = 8
+FRONT_TILES = 2
+PAGES = 4
 M_TILES = M // P
 FLOPS = 2 * K * M * S
 
@@ -29,6 +31,7 @@ def tile_list_hboth_gelu_kernel(tc, xT, w_words, w_scales, wgt, b, wgo, offs, of
     with ExitStack() as ctx:
         lists = ctx.enter_context(tc.tile_pool(name="lists", bufs=1))
         keep = ctx.enter_context(tc.tile_pool(name="keep", bufs=1))
+        pages = ctx.enter_context(tc.tile_pool(name="pages", bufs=PAGES))
         psum = ctx.enter_context(tc.psum_pool(name="psum", bufs=6))
         turn = ctx.enter_context(tc.psum_pool(name="turn", bufs=1))
 
@@ -36,7 +39,8 @@ def tile_list_hboth_gelu_kernel(tc, xT, w_words, w_scales, wgt, b, wgo, offs, of
         places = lists.tile([P, S // 16], U16, name="places")
         wgt_all = keep.tile([P, S], F32, name="wgt_all")
         planes = [keep.tile([P, T], F32, name=f"plane{i}") for i in range(PACK)]
-        w_codes = keep.tile([P, 2 * M], U8, name="w_codes", align_bytes=64)
+        w_front = keep.tile([P, 2 * P * FRONT_TILES], U8, name="w_front", align_bytes=64)
+        w_back = keep.tile([P, 2 * (M - P * FRONT_TILES)], U8, name="w_back", align_bytes=64)
         w_plane = keep.tile([P, M], U8, name="w_plane", align_bytes=64)
         wgo_all = keep.tile([P, S], F32, name="wgo_all")
         b_rows = keep.tile([P, P], F32, name="b_rows")
@@ -44,7 +48,7 @@ def tile_list_hboth_gelu_kernel(tc, xT, w_words, w_scales, wgt, b, wgo, offs, of
         identity = keep.tile([P, P], F32, name="identity")
         b_turned = turn.tile([P, P], F32, name="b_turned")
         warm_out = keep.tile([P, 8], F32, name="warm_out")
-        rows = [keep.tile([P, T], F32, name=f"rows{m}") for m in range(M_TILES)]
+        rows = [pages.tile([P, T], F32, name="rows") for m in range(PAGES)]
 
         nc.gpsimd.memset(b_rows[:], 0.0)
         nc.scalar.dma_start(out=b_rows[0:M_TILES, :], in_=b.rearrange("(m p) -> m p", p=P))
@@ -67,13 +71,14 @@ def tile_list_hboth_gelu_kernel(tc, xT, w_words, w_scales, wgt, b, wgo, offs, of
                 out=w_plane[32 * q : 32 * q + 4, :].bitcast(I32),
                 in_=w_scales[0, 4 * q : 4 * q + 4, :].bitcast(I32),
             )
-        nc.sync.dma_start(out=w_codes[:].bitcast(I32), in_=w_words[0].bitcast(I32))
+        nc.sync.dma_start(out=w_front[:].bitcast(I32), in_=w_words[0, :, 0 : 2 * P * FRONT_TILES].bitcast(I32))
         make_identity(nc, identity[:])
         nc.tensor.transpose(b_turned[:], b_rows[:], identity[:])
         nc.sync.dma_start(out=wgo_all[:], in_=wgo)
         nc.sync.dma_start(places[:], offs2)
+        nc.sync.dma_start(out=w_back[:].bitcast(I32), in_=w_words[0, :, 2 * P * FRONT_TILES : 2 * M].bitcast(I32))
 
-        for m in range(M_TILES):
+        for m in range(PAGES):
             if m < 2:
                 nc.vector.memset(rows[m][:].bitcast(I32), 0)
             else:
@@ -114,13 +119,17 @@ def tile_list_hboth_gelu_kernel(tc, xT, w_words, w_scales, wgt, b, wgo, offs, of
         def quantize(cols):
             nc.vector.quantize_mx(out=codes[:, cols].bitcast(FP8X4), scales=scales[:, cols], in_=grouped(cols))
 
+        def weights(m):
+            tile, n = (w_front, m) if m < FRONT_TILES else (w_back, m - FRONT_TILES)
+            return tile[:, 2 * P * n : 2 * P * (n + 1)]
+
         def project(m, parts, result, bias):
             start, stop = parts[0].start, parts[-1].stop
             acc = psum.tile([P, stop - start], F32, name="acc")
             for cols in parts:
                 nc.tensor.matmul_mx(
                     out=acc[:, cols.start - start : cols.stop - start],
-                    lhsT=w_codes[:, 2 * P * m : 2 * P * (m + 1)].bitcast(FP4X4),
+                    lhsT=weights(m).bitcast(FP4X4),
                     lhsT_scale=w_plane[:, P * m : P * (m + 1)],
                     rhs=codes[:, cols].bitcast(FP8X4),
                     rhs_scale=scales[:, cols],
@@ -172,6 +181,9 @@ def tile_list_hboth_gelu_kernel(tc, xT, w_words, w_scales, wgt, b, wgo, offs, of
         place(2, last, results[2][:, last])
         store(2)
         for m in range(3, M_TILES):
+            if m >= PAGES:
+                rows.append(pages.tile([P, T], F32, name="rows"))
+                nc.gpsimd.memset(rows[m][:].bitcast(I32), 0)
             project(m, [whole], results[m][:], b_cols[:, m : m + 1])
             place(m, whole, results[m][:])
             store(m)

@@ -10,7 +10,7 @@ HALF = S // 2
 QUARTER = S // 4
 OVERHANG = 8
 FRONT_TILES = 2
-PAGES = 4
+PAGES = 6
 M_TILES = M // P
 FLOPS = 2 * K * M * S
 
@@ -79,7 +79,7 @@ def tile_list_hboth_gelu_kernel(tc, xT, w_words, w_scales, wgt, b, wgo, offs, of
         nc.sync.dma_start(out=w_back[:].bitcast(I32), in_=w_words[0, :, 2 * P * FRONT_TILES : 2 * M].bitcast(I32))
 
         for m in range(PAGES):
-            if m < 2:
+            if m < PAGES // 2:
                 nc.vector.memset(rows[m][:].bitcast(I32), 0)
             else:
                 nc.gpsimd.memset(rows[m][:].bitcast(I32), 0)
@@ -144,7 +144,7 @@ def tile_list_hboth_gelu_kernel(tc, xT, w_words, w_scales, wgt, b, wgo, offs, of
         def store(m):
             nc.sync.dma_start(out=out[P * m : P * (m + 1), :], in_=rows[m][:])
 
-        low_pair, high_pair, all_four = slice(0, 2), slice(2, PACK), slice(0, PACK)
+        low_pair, high_pair = slice(0, 2), slice(2, PACK)
         nc.scalar.copy(out=b_cols[:], in_=b_turned[:, 0:M_TILES])
         first_bias = grouped_last[:].bitcast(F32)[:, 0:2]
         nc.scalar.copy(out=first_bias, in_=b_turned[:, 0:2])
@@ -169,7 +169,10 @@ def tile_list_hboth_gelu_kernel(tc, xT, w_words, w_scales, wgt, b, wgo, offs, of
         quantize(middle)
         for m in range(2):
             place(m, first, results[m][:, first])
-        group(last, all_four, picked_last)
+        nc.scalar.copy(
+            out=grouped_last[:].rearrange("p (c i t) -> p c t i", i=4, t=PACK),
+            in_=picked_last.rearrange("p t (c i) -> p c t i", i=4),
+        )
         quantize(last)
         project(2, [first, middle], reused[:, early], b_cols[:, 2:3])
         place(2, early, reused[:, early])

@@ -10,7 +10,7 @@ HALF = S // 2
 QUARTER = S // 4
 OVERHANG = 8
 FRONT_TILES = 2
-PAGES = 6
+PAGES = 3
 M_TILES = M // P
 FLOPS = 2 * K * M * S
 
@@ -31,7 +31,6 @@ def tile_list_hboth_gelu_kernel(tc, xT, w_words, w_scales, wgt, b, wgo, offs, of
     with ExitStack() as ctx:
         lists = ctx.enter_context(tc.tile_pool(name="lists", bufs=1))
         keep = ctx.enter_context(tc.tile_pool(name="keep", bufs=1))
-        pages = ctx.enter_context(tc.tile_pool(name="pages", bufs=PAGES))
         psum = ctx.enter_context(tc.psum_pool(name="psum", bufs=6))
         turn = ctx.enter_context(tc.psum_pool(name="turn", bufs=1))
 
@@ -48,7 +47,8 @@ def tile_list_hboth_gelu_kernel(tc, xT, w_words, w_scales, wgt, b, wgo, offs, of
         identity = keep.tile([P, P], F32, name="identity")
         b_turned = turn.tile([P, P], F32, name="b_turned")
         warm_out = keep.tile([P, 8], F32, name="warm_out")
-        rows = [pages.tile([P, T], F32, name="rows") for m in range(PAGES)]
+        pages = [keep.tile([P, T], F32, name=f"page{n}") for n in range(PAGES)]
+        rows = [pages[m % PAGES] for m in range(M_TILES)]
 
         nc.gpsimd.memset(b_rows[:], 0.0)
         nc.scalar.dma_start(out=b_rows[0:M_TILES, :], in_=b.rearrange("(m p) -> m p", p=P))
@@ -78,11 +78,8 @@ def tile_list_hboth_gelu_kernel(tc, xT, w_words, w_scales, wgt, b, wgo, offs, of
         nc.sync.dma_start(places[:], offs2)
         nc.sync.dma_start(out=w_back[:].bitcast(I32), in_=w_words[0, :, 2 * P * FRONT_TILES : 2 * M].bitcast(I32))
 
-        for m in range(PAGES):
-            if m < PAGES // 2:
-                nc.vector.memset(rows[m][:].bitcast(I32), 0)
-            else:
-                nc.gpsimd.memset(rows[m][:].bitcast(I32), 0)
+        for page in pages:
+            nc.vector.memset(page[:].bitcast(I32), 0)
 
         codes = keep.tile([P, S], U32, name="codes", align_bytes=64)
         scales = keep.tile([P, S], U8, name="scales", align_bytes=64)
@@ -184,9 +181,6 @@ def tile_list_hboth_gelu_kernel(tc, xT, w_words, w_scales, wgt, b, wgo, offs, of
         place(2, last, results[2][:, last])
         store(2)
         for m in range(3, M_TILES):
-            if m >= PAGES:
-                rows.append(pages.tile([P, T], F32, name="rows"))
-                nc.gpsimd.memset(rows[m][:].bitcast(I32), 0)
             project(m, [whole], results[m][:], b_cols[:, m : m + 1])
             place(m, whole, results[m][:])
             store(m)

@@ -10,7 +10,7 @@ HALF = S // 2
 QUARTER = S // 4
 OVERHANG = 8
 FRONT_TILES = 2
-PAGES = 3
+PAGES = 4
 M_TILES = M // P
 FLOPS = 2 * K * M * S
 
@@ -78,8 +78,9 @@ def tile_list_hboth_gelu_kernel(tc, xT, w_words, w_scales, wgt, b, wgo, offs, of
         nc.sync.dma_start(places[:], offs2)
         nc.sync.dma_start(out=w_back[:].bitcast(I32), in_=w_words[0, :, 2 * P * FRONT_TILES : 2 * M].bitcast(I32))
 
-        for page in pages:
+        for page in pages[:-1]:
             nc.vector.memset(page[:].bitcast(I32), 0)
+        nc.gpsimd.memset(pages[-1][:].bitcast(I32), 0)
 
         codes = keep.tile([P, S], U32, name="codes", align_bytes=64)
         scales = keep.tile([P, S], U8, name="scales", align_bytes=64)

@@ -51,7 +51,6 @@ def tile_list_hboth_gelu_kernel(tc, xT, w_words, w_scales, wgt, b, wgo, offs, of
         rows = [pages[m % PAGES] for m in range(M_TILES)]
 
         nc.gpsimd.memset(b_rows[:], 0.0)
-        nc.scalar.dma_start(out=b_rows[0:M_TILES, :], in_=b.rearrange("(m p) -> m p", p=P))
         nc.scalar.activation(warm_out[64:P, :], b_rows[64:P, 0:8], GELU)
         nc.gpsimd.memset(w_plane[:].bitcast(I32), 0)
 
@@ -66,6 +65,7 @@ def tile_list_hboth_gelu_kernel(tc, xT, w_words, w_scales, wgt, b, wgo, offs, of
         for i in range(1, PACK):
             nc.sync.dma_start(out=planes[i][:], in_=x_planes[:, i, :])
         nc.sync.dma_start(out=wgt_all[:, last], in_=wgt[:, last])
+        nc.sync.dma_start(out=b_rows[0:M_TILES, :], in_=b.rearrange("(m p) -> m p", p=P))
         for q in range(4):
             nc.sync.dma_start(
                 out=w_plane[32 * q : 32 * q + 4, :].bitcast(I32),

@@ -6,6 +6,8 @@ from concourse.masks import make_identity
 K, M, T, S = 512, 1024, 1024, 512
 P = 128
 PACK = 4
+BLOCK = 32
+GROUP = 16
 HALF = S // 2
 QUARTER = S // 4
 OVERHANG = 8
@@ -33,10 +35,15 @@ def tile_list_hboth_gelu_kernel(tc, xT, w_words, w_scales, wgt, b, wgo, offs, of
         keep = ctx.enter_context(tc.tile_pool(name="keep", bufs=1))
         psum = ctx.enter_context(tc.psum_pool(name="psum", bufs=6))
         turn = ctx.enter_context(tc.psum_pool(name="turn", bufs=1))
+        late = ctx.enter_context(tc.tile_pool(name="late", bufs=1))
 
         picks = lists.tile([P, S // 16], U16, name="picks")
         places = lists.tile([P, S // 16], U16, name="places")
-        wgt_all = keep.tile([P, S], F32, name="wgt_all")
+        wgt_all = keep.tile([P, S], F32, name="wgt_all", align_bytes=64)
+        wgt_dealt = keep.tile([P, BLOCK], F32, name="wgt_dealt", align_bytes=64)
+        wgt_turned = keep.tile([P, BLOCK], F32, name="wgt_turned", align_bytes=64)
+        repeated_front = keep.tile([P, HALF], F32, name="repeated_front", align_bytes=64)
+        repeated_third = late.tile([P, QUARTER], F32, name="repeated_third", offset=4 * T - 2 * QUARTER, align_bytes=64)
         planes = [keep.tile([P, T], F32, name=f"plane{i}") for i in range(PACK)]
         w_front = keep.tile([P, 2 * P * FRONT_TILES], U8, name="w_front", align_bytes=64)
         w_back = keep.tile([P, 2 * (M - P * FRONT_TILES)], U8, name="w_back", align_bytes=64)
@@ -47,7 +54,8 @@ def tile_list_hboth_gelu_kernel(tc, xT, w_words, w_scales, wgt, b, wgo, offs, of
         identity = keep.tile([P, P], F32, name="identity")
         b_turned = turn.tile([P, P], F32, name="b_turned")
         warm_out = keep.tile([P, 8], F32, name="warm_out")
-        pages = [keep.tile([P, T], F32, name=f"page{n}") for n in range(PAGES)]
+        pages = [keep.tile([P, T], F32, name=f"page{n}") for n in range(2)]
+        pages = pages + [late.tile([P, T], F32, name=f"late_page{n}", offset=4 * T * n) for n in range(PAGES - 2)]
         rows = [pages[m % PAGES] for m in range(M_TILES)]
 
         nc.gpsimd.memset(b_rows[:], 0.0)
@@ -56,12 +64,13 @@ def tile_list_hboth_gelu_kernel(tc, xT, w_words, w_scales, wgt, b, wgo, offs, of
 
         first, middle, last = slice(0, QUARTER), slice(QUARTER, S - QUARTER), slice(S - QUARTER, S)
         early, rest, whole = slice(0, S - QUARTER), slice(QUARTER, S), slice(0, S)
-        front, back, third = slice(0, HALF), slice(HALF, S), slice(HALF, S - QUARTER)
+        front, third = slice(0, HALF), slice(HALF, S - QUARTER)
 
         x_planes = xT.rearrange("(p i) t -> p i t", i=PACK)
+        half_rows = wgt.rearrange("r (h c) -> (r h) c", h=2)[0 : 2 * P : GROUP + 1, :]
+        nc.sync.dma_start(out=wgt_dealt[:], in_=half_rows.rearrange("u (v c) -> u v c", c=BLOCK))
         nc.sync.dma_start(out=planes[0][:], in_=x_planes[:, 0, :])
         nc.sync.dma_start(picks[:], offs)
-        nc.sync.dma_start(out=wgt_all[:, early], in_=wgt[:, early])
         for i in range(1, PACK):
             nc.sync.dma_start(out=planes[i][:], in_=x_planes[:, i, :])
         nc.sync.dma_start(out=wgt_all[:, last], in_=wgt[:, last])
@@ -78,15 +87,27 @@ def tile_list_hboth_gelu_kernel(tc, xT, w_words, w_scales, wgt, b, wgo, offs, of
         nc.sync.dma_start(places[:], offs2)
         nc.sync.dma_start(out=w_back[:].bitcast(I32), in_=w_words[0, :, 2 * P * FRONT_TILES : 2 * M].bitcast(I32))
 
-        for page in pages[:-1]:
+        for page in pages[:2]:
             nc.vector.memset(page[:].bitcast(I32), 0)
-        nc.gpsimd.memset(pages[-1][:].bitcast(I32), 0)
+
+        nc.vector.transpose(wgt_turned[:], wgt_dealt[:])
+        by_block = wgt_turned[:].rearrange("p (h k) -> p k h", h=2)
+        spread = [(front, repeated_front), (third, repeated_third)]
+        for cols, repeated in spread:
+            blocks = (cols.stop - cols.start) // BLOCK
+            nc.vector.tensor_copy(
+                repeated[:].rearrange("p (k h r) -> p k h r", h=2, r=GROUP),
+                by_block[:, cols.start // BLOCK : cols.stop // BLOCK, :].unsqueeze(3).to_broadcast([P, blocks, 2, GROUP]),
+            )
+        for cols, repeated in spread:
+            nc.vector.transpose(wgt_all[:, cols], repeated[:])
+        for page in pages[2:]:
+            nc.gpsimd.memset(page[:].bitcast(I32), 0)
 
         codes = keep.tile([P, S], U32, name="codes", align_bytes=64)
         scales = keep.tile([P, S], U8, name="scales", align_bytes=64)
         low = keep.tile([P, 2, S - QUARTER], F32, name="low")
         high_middle = keep.tile([P, 2, HALF], F32, name="high_middle")
-        unweighted = keep.tile([P, HALF], F32, name="unweighted")
         reused = keep.tile([P, S], F32, name="reused")
         high_first = reused[:, 0 : 2 * (QUARTER + OVERHANG)].rearrange("p (t c) -> p t c", t=2)[:, :, 0:QUARTER]
         picked_last = reused[:].rearrange("p (t c) -> p t c", t=PACK)
@@ -104,9 +125,6 @@ def tile_list_hboth_gelu_kernel(tc, xT, w_words, w_scales, wgt, b, wgo, offs, of
 
         def gather(i, cols, dst):
             nc.vector.tensor_tensor(dst, planes[i][:].indirect(entries(picks, cols)), wgt_all[:, cols], MULT)
-
-        def weigh(cols, dst):
-            nc.vector.tensor_tensor(dst, unweighted[:, cols.start - HALF : cols.stop - HALF], wgt_all[:, cols], MULT)
 
         def group(cols, which, src):
             nc.scalar.copy(
@@ -146,10 +164,8 @@ def tile_list_hboth_gelu_kernel(tc, xT, w_words, w_scales, wgt, b, wgo, offs, of
         nc.scalar.copy(out=b_cols[:], in_=b_turned[:, 0:M_TILES])
         first_bias = grouped_last[:].bitcast(F32)[:, 0:2]
         nc.scalar.copy(out=first_bias, in_=b_turned[:, 0:2])
-        nc.vector.tensor_copy(unweighted[:], planes[0][:].indirect(entries(picks, back)))
-        gather(0, front, low[:, 0, front])
-        weigh(third, low[:, 0, third])
-        gather(1, early, low[:, 1, :])
+        for i in range(2):
+            gather(i, early, low[:, i, :])
         group(early, low_pair, low[:])
         gather(2, first, high_first[:, 0, :])
         gather(2, middle, high_middle[:, 0, :])
@@ -161,9 +177,8 @@ def tile_list_hboth_gelu_kernel(tc, xT, w_words, w_scales, wgt, b, wgo, offs, of
         quantize(first)
         for m in range(2):
             project(m, [first], results[m][:, first], first_bias[:, m : m + 1])
-        for i in range(1, 3):
+        for i in range(3):
             gather(i, last, picked_last[:, i, :])
-        weigh(last, picked_last[:, 0, :])
         quantize(middle)
         for m in range(2):
             place(m, first, results[m][:, first])

@@ -10,7 +10,6 @@ BLOCK = 32
 GROUP = 16
 HALF = S // 2
 QUARTER = S // 4
-OVERHANG = 8
 FRONT_TILES = 2
 PAGES = 4
 M_TILES = M // P
@@ -43,7 +42,7 @@ def tile_list_hboth_gelu_kernel(tc, xT, w_words, w_scales, wgt, b, wgo, offs, of
         wgt_dealt = keep.tile([P, BLOCK], F32, name="wgt_dealt", align_bytes=64)
         wgt_turned = keep.tile([P, BLOCK], F32, name="wgt_turned", align_bytes=64)
         repeated_front = keep.tile([P, HALF], F32, name="repeated_front", align_bytes=64)
-        repeated_third = late.tile([P, QUARTER], F32, name="repeated_third", offset=4 * T - 2 * QUARTER, align_bytes=64)
+        repeated_back = late.tile([P, HALF], F32, name="repeated_back", offset=4 * T - 2 * HALF, align_bytes=64)
         planes = [keep.tile([P, T], F32, name=f"plane{i}") for i in range(PACK)]
         w_front = keep.tile([P, 2 * P * FRONT_TILES], U8, name="w_front", align_bytes=64)
         w_back = keep.tile([P, 2 * (M - P * FRONT_TILES)], U8, name="w_back", align_bytes=64)
@@ -64,7 +63,7 @@ def tile_list_hboth_gelu_kernel(tc, xT, w_words, w_scales, wgt, b, wgo, offs, of
 
         first, middle, last = slice(0, QUARTER), slice(QUARTER, S - QUARTER), slice(S - QUARTER, S)
         early, rest, whole = slice(0, S - QUARTER), slice(QUARTER, S), slice(0, S)
-        front, third = slice(0, HALF), slice(HALF, S - QUARTER)
+        front, back = slice(0, HALF), slice(HALF, S)
 
         x_planes = xT.rearrange("(p i) t -> p i t", i=PACK)
         half_rows = wgt.rearrange("r (h c) -> (r h) c", h=2)[0 : 2 * P : GROUP + 1, :]
@@ -73,7 +72,6 @@ def tile_list_hboth_gelu_kernel(tc, xT, w_words, w_scales, wgt, b, wgo, offs, of
         nc.sync.dma_start(picks[:], offs)
         for i in range(1, PACK):
             nc.sync.dma_start(out=planes[i][:], in_=x_planes[:, i, :])
-        nc.sync.dma_start(out=wgt_all[:, last], in_=wgt[:, last])
         nc.sync.dma_start(out=b_rows[0:M_TILES, :], in_=b.rearrange("(m p) -> m p", p=P))
         for q in range(4):
             nc.sync.dma_start(
@@ -92,7 +90,7 @@ def tile_list_hboth_gelu_kernel(tc, xT, w_words, w_scales, wgt, b, wgo, offs, of
 
         nc.vector.transpose(wgt_turned[:], wgt_dealt[:])
         by_block = wgt_turned[:].rearrange("p (h k) -> p k h", h=2)
-        spread = [(front, repeated_front), (third, repeated_third)]
+        spread = [(front, repeated_front), (back, repeated_back)]
         for cols, repeated in spread:
             blocks = (cols.stop - cols.start) // BLOCK
             nc.vector.tensor_copy(
@@ -106,11 +104,13 @@ def tile_list_hboth_gelu_kernel(tc, xT, w_words, w_scales, wgt, b, wgo, offs, of
 
         codes = keep.tile([P, S], U32, name="codes", align_bytes=64)
         scales = keep.tile([P, S], U8, name="scales", align_bytes=64)
-        low = keep.tile([P, 2, S - QUARTER], F32, name="low")
+        pitch = S + 3 * QUARTER
+        picked = keep.tile([P, 2 * pitch], F32, name="picked")
+        low = picked[:].rearrange("p (t c) -> p t c", t=2)
         high_middle = keep.tile([P, 2, HALF], F32, name="high_middle")
-        reused = keep.tile([P, S], F32, name="reused")
-        high_first = reused[:, 0 : 2 * (QUARTER + OVERHANG)].rearrange("p (t c) -> p t c", t=2)[:, :, 0:QUARTER]
-        picked_last = reused[:].rearrange("p (t c) -> p t c", t=PACK)
+        high_first = picked[:, S : S + HALF].rearrange("p (t c) -> p t c", t=2)
+        picked_last = picked[:, last.start : pitch].rearrange("p (t c) -> p t c", t=PACK)
+        reused = picked[:, S:pitch]
         grouped_early = keep.tile([P, (S - QUARTER) * PACK], BF16, name="grouped_early", align_bytes=64)
         grouped_last = keep.tile([P, QUARTER * PACK], BF16, name="grouped_last", align_bytes=64)
         results = [keep.tile([P, S], F32, name=f"result{m}") for m in range(M_TILES)]
@@ -164,9 +164,10 @@ def tile_list_hboth_gelu_kernel(tc, xT, w_words, w_scales, wgt, b, wgo, offs, of
         nc.scalar.copy(out=b_cols[:], in_=b_turned[:, 0:M_TILES])
         first_bias = grouped_last[:].bitcast(F32)[:, 0:2]
         nc.scalar.copy(out=first_bias, in_=b_turned[:, 0:2])
-        for i in range(2):
-            gather(i, early, low[:, i, :])
-        group(early, low_pair, low[:])
+        for cols in (front, back):
+            gather(0, cols, low[:, 0, cols])
+        gather(1, early, low[:, 1, early])
+        group(early, low_pair, low[:, :, early])
         gather(2, first, high_first[:, 0, :])
         gather(2, middle, high_middle[:, 0, :])
         gather(3, first, high_first[:, 1, :])
@@ -177,7 +178,7 @@ def tile_list_hboth_gelu_kernel(tc, xT, w_words, w_scales, wgt, b, wgo, offs, of
         quantize(first)
         for m in range(2):
             project(m, [first], results[m][:, first], first_bias[:, m : m + 1])
-        for i in range(3):
+        for i in range(1, 3):
             gather(i, last, picked_last[:, i, :])
         quantize(middle)
         for m in range(2):
@@ -187,8 +188,8 @@ def tile_list_hboth_gelu_kernel(tc, xT, w_words, w_scales, wgt, b, wgo, offs, of
             in_=picked_last.rearrange("p t (c i) -> p c t i", i=4),
         )
         quantize(last)
-        project(2, [first, middle], reused[:, early], b_cols[:, 2:3])
-        place(2, early, reused[:, early])
+        project(2, [first, middle], reused, b_cols[:, 2:3])
+        place(2, early, reused)
         for m in range(2):
             project(m, [middle, last], results[m][:, rest], b_cols[:, m : m + 1])
             place(m, rest, results[m][:, rest])

from contextlib import ExitStack

import concourse.mybir as mybir
from concourse.masks import make_identity

K, M, T, S = 512, 1024, 1024, 512
P = 128
PACK = 4
BLOCK = 32
GROUP = 16
HALF = S // 2
QUARTER = S // 4
FRONT_TILES = 2
PAGES = 4
M_TILES = M // P
FLOPS = 2 * K * M * S

F32 = mybir.dt.float32
BF16 = mybir.dt.bfloat16
I32 = mybir.dt.int32
U32 = mybir.dt.uint32
U16 = mybir.dt.uint16
U8 = mybir.dt.uint8
FP8X4 = mybir.dt.float8_e4m3fn_x4
FP4X4 = mybir.dt.float4_e2m1fn_x4
MULT = mybir.AluOpType.mult
GELU = mybir.ActivationFunctionType.Gelu_apprx_tanh


def tile_list_hboth_gelu_kernel(tc, xT, w_words, w_scales, wgt, b, wgo, offs, offs2, out):
    nc = tc.nc
    with ExitStack() as ctx:
        lists = ctx.enter_context(tc.tile_pool(name="lists", bufs=1))
        keep = ctx.enter_context(tc.tile_pool(name="keep", bufs=1))
        psum = ctx.enter_context(tc.psum_pool(name="psum", bufs=6))
        turn = ctx.enter_context(tc.psum_pool(name="turn", bufs=1))
        late = ctx.enter_context(tc.tile_pool(name="late", bufs=1))

        picks = lists.tile([P, S // 16], U16, name="picks")
        places = lists.tile([P, S // 16], U16, name="places")
        wgt_all = keep.tile([P, S], F32, name="wgt_all", align_bytes=64)
        wgt_dealt = keep.tile([P, BLOCK], F32, name="wgt_dealt", align_bytes=64)
        wgt_turned = keep.tile([P, BLOCK], F32, name="wgt_turned", align_bytes=64)
        repeated_front = keep.tile([P, HALF], F32, name="repeated_front", align_bytes=64)
        repeated_back = late.tile([P, HALF], F32, name="repeated_back", offset=4 * T - 2 * HALF, align_bytes=64)
        planes = [keep.tile([P, T], F32, name=f"plane{i}") for i in range(PACK)]
        w_front = keep.tile([P, 2 * P * FRONT_TILES], U8, name="w_front", align_bytes=64)
        w_back = keep.tile([P, 2 * (M - P * FRONT_TILES)], U8, name="w_back", align_bytes=64)
        w_plane = keep.tile([P, M], U8, name="w_plane", align_bytes=64)
        wgo_all = keep.tile([P, S], F32, name="wgo_all")
        b_rows = keep.tile([P, P], F32, name="b_rows")
        b_cols = keep.tile([P, M_TILES], F32, name="b_cols")
        identity = keep.tile([P, P], F32, name="identity")
        b_turned = turn.tile([P, P], F32, name="b_turned")
        warm_out = keep.tile([P, 8], F32, name="warm_out")
        pages = [keep.tile([P, T], F32, name=f"page{n}") for n in range(2)]
        pages = pages + [late.tile([P, T], F32, name=f"late_page{n}", offset=4 * T * n) for n in range(PAGES - 2)]
        rows = [pages[m % PAGES] for m in range(M_TILES)]

        nc.gpsimd.memset(b_rows[:], 0.0)
        nc.scalar.activation(warm_out[64:P, :], b_rows[64:P, 0:8], GELU)
        nc.gpsimd.memset(w_plane[:].bitcast(I32), 0)

        first, middle, last = slice(0, QUARTER), slice(QUARTER, S - QUARTER), slice(S - QUARTER, S)
        early, rest, whole = slice(0, S - QUARTER), slice(QUARTER, S), slice(0, S)
        front, back = slice(0, HALF), slice(HALF, S)

        x_planes = xT.rearrange("(p i) t -> p i t", i=PACK)
        half_rows = wgt.rearrange("r (h c) -> (r h) c", h=2)[0 : 2 * P : GROUP + 1, :]
        nc.sync.dma_start(out=wgt_dealt[:], in_=half_rows.rearrange("u (v c) -> u v c", c=BLOCK))
        nc.sync.dma_start(out=planes[0][:], in_=x_planes[:, 0, :])
        nc.sync.dma_start(picks[:], offs)
        for i in range(1, PACK):
            nc.sync.dma_start(out=planes[i][:], in_=x_planes[:, i, :])
        nc.sync.dma_start(out=b_rows[0:M_TILES, :], in_=b.rearrange("(m p) -> m p", p=P))
        for q in range(4):
            nc.sync.dma_start(
                out=w_plane[32 * q : 32 * q + 4, :].bitcast(I32),
                in_=w_scales[0, 4 * q : 4 * q + 4, :].bitcast(I32),
            )
        nc.sync.dma_start(out=w_front[:].bitcast(I32), in_=w_words[0, :, 0 : 2 * P * FRONT_TILES].bitcast(I32))
        make_identity(nc, identity[:])
        nc.tensor.transpose(b_turned[:], b_rows[:], identity[:])
        nc.sync.dma_start(out=wgo_all[:], in_=wgo)
        nc.sync.dma_start(places[:], offs2)
        nc.sync.dma_start(out=w_back[:].bitcast(I32), in_=w_words[0, :, 2 * P * FRONT_TILES : 2 * M].bitcast(I32))

        for page in pages[:2]:
            nc.vector.memset(page[:].bitcast(I32), 0)

        nc.vector.transpose(wgt_turned[:], wgt_dealt[:])
        by_block = wgt_turned[:].rearrange("p (h k) -> p k h", h=2)
        spread = [(front, repeated_front), (back, repeated_back)]
        for cols, repeated in spread:
            blocks = (cols.stop - cols.start) // BLOCK
            nc.vector.tensor_copy(
                repeated[:].rearrange("p (k h r) -> p k h r", h=2, r=GROUP),
                by_block[:, cols.start // BLOCK : cols.stop // BLOCK, :].unsqueeze(3).to_broadcast([P, blocks, 2, GROUP]),
            )
        for cols, repeated in spread:
            nc.vector.transpose(wgt_all[:, cols], repeated[:])
        for page in pages[2:]:
            nc.gpsimd.memset(page[:].bitcast(I32), 0)

        codes = keep.tile([P, S], U32, name="codes", align_bytes=64)
        scales = keep.tile([P, S], U8, name="scales", align_bytes=64)
        pitch = S + 3 * QUARTER
        picked = keep.tile([P, 2 * pitch], F32, name="picked")
        low = picked[:].rearrange("p (t c) -> p t c", t=2)
        high_middle = keep.tile([P, 2, HALF], F32, name="high_middle")
        high_first = picked[:, S : S + HALF].rearrange("p (t c) -> p t c", t=2)
        picked_last = picked[:, last.start : pitch].rearrange("p (t c) -> p t c", t=PACK)
        reused = picked[:, S:pitch]
        grouped_early = keep.tile([P, (S - QUARTER) * PACK], BF16, name="grouped_early", align_bytes=64)
        grouped_last = keep.tile([P, QUARTER * PACK], BF16, name="grouped_last", align_bytes=64)
        results = [keep.tile([P, S], F32, name=f"result{m}") for m in range(M_TILES)]

        def grouped(cols):
            if cols == last:
                return grouped_last[:]
            return grouped_early[:, cols.start * PACK : cols.stop * PACK]

        def entries(tile, cols):
            return tile[:, cols.start // 16 : cols.stop // 16]

        def gather(i, cols, dst):
            nc.vector.tensor_tensor(dst, planes[i][:].indirect(entries(picks, cols)), wgt_all[:, cols], MULT)

        def group(cols, which, src):
            nc.scalar.copy(
                out=grouped(cols).rearrange("p (c t) -> p c t", t=PACK)[:, :, which],
                in_=src.rearrange("p t c -> p c t"),
            )

        def quantize(cols):
            nc.vector.quantize_mx(out=codes[:, cols].bitcast(FP8X4), scales=scales[:, cols], in_=grouped(cols))

        def weights(m):
            tile, n = (w_front, m) if m < FRONT_TILES else (w_back, m - FRONT_TILES)
            return tile[:, 2 * P * n : 2 * P * (n + 1)]

        def project(m, parts, result, bias):
            start, stop = parts[0].start, parts[-1].stop
            acc = psum.tile([P, stop - start], F32, name="acc")
            for cols in parts:
                nc.tensor.matmul_mx(
                    out=acc[:, cols.start - start : cols.stop - start],
                    lhsT=weights(m).bitcast(FP4X4),
                    lhsT_scale=w_plane[:, P * m : P * (m + 1)],
                    rhs=codes[:, cols].bitcast(FP8X4),
                    rhs_scale=scales[:, cols],
                    start=True,
                    stop=True,
                )
            nc.scalar.activation(result, acc[:], GELU, bias=bias)

        def place(m, cols, result):
            nc.vector.tensor_tensor(rows[m][:].indirect(entries(places, cols)), result, wgo_all[:, cols], MULT)

        def store(m):
            nc.sync.dma_start(out=out[P * m : P * (m + 1), :], in_=rows[m][:])

        low_pair, high_pair = slice(0, 2), slice(2, PACK)
        nc.scalar.copy(out=b_cols[:], in_=b_turned[:, 0:M_TILES])
        first_bias = grouped_last[:].bitcast(F32)[:, 0:2]
        nc.scalar.copy(out=first_bias, in_=b_turned[:, 0:2])
        for cols in (front, back):
            gather(0, cols, low[:, 0, cols])
        gather(1, early, low[:, 1, early])
        group(early, low_pair, low[:, :, early])
        gather(2, first, high_first[:, 0, :])
        gather(2, middle, high_middle[:, 0, :])
        gather(3, first, high_first[:, 1, :])
        group(first, high_pair, high_first)
        gather(3, middle, high_middle[:, 1, :])
        group(middle, high_pair, high_middle[:])
        gather(3, last, picked_last[:, 3, :])
        quantize(first)
        for m in range(2):
            project(m, [first], results[m][:, first], first_bias[:, m : m + 1])
        for i in range(1, 3):
            gather(i, last, picked_last[:, i, :])
        quantize(middle)
        for m in range(2):
            place(m, first, results[m][:, first])
        nc.scalar.copy(
            out=grouped_last[:].rearrange("p (c i t) -> p c t i", i=4, t=PACK),
            in_=picked_last.rearrange("p t (c i) -> p c t i", i=4),
        )
        quantize(last)
        project(2, [first, middle], reused, b_cols[:, 2:3])
        place(2, early, reused)
        for m in range(2):
            project(m, [middle, last], results[m][:, rest], b_cols[:, m : m + 1])
            place(m, rest, results[m][:, rest])
            store(m)
        project(2, [last], results[2][:, last], b_cols[:, 2:3])
        place(2, last, results[2][:, last])
        store(2)
        for m in range(3, M_TILES):
            project(m, [whole], results[m][:], b_cols[:, m : m + 1])
            place(m, whole, results[m][:])
            store(m)
